import numpy as np
import ml_dtypes


def mxq(x, axis, fmt="e4m3"):
    dtype, down = {"e4m3": (ml_dtypes.float8_e4m3fn, 7), "e5m2": (ml_dtypes.float8_e5m2, 14)}[fmt]
    v = np.moveaxis(np.asarray(x, np.float32).astype(ml_dtypes.bfloat16).astype(np.float64), axis, -1)
    blocks = v.reshape(v.shape[:-1] + (-1, 32))
    amax = np.abs(blocks).max(-1, keepdims=True)
    byte = np.maximum(np.where(amax > 0, np.frexp(amax)[1] - 1 + 127, 0) - down, 1)
    scale = np.exp2(byte - 127.0)
    codes = (blocks / scale).astype(np.float32).astype(dtype).astype(np.float64)
    return np.moveaxis((codes * scale).reshape(v.shape), -1, axis)


WIDE = False


def mx_kscale(k):
    if not WIDE:
        return np.ones(k)
    levels = np.array([10, -10, 5, -5, 0])
    if k % 512:
        return np.exp2(np.random.permutation(np.resize(levels, k // 32))).repeat(32)
    a = np.empty((k // 512, 16))
    for p in range(k // 512):
        a[p, :8] = np.random.permutation(np.resize(levels, 8))
        for g in range(8):
            far = levels[np.abs(levels - a[p, g]) >= 10]
            a[p, g + 8] = far[np.random.randint(len(far))]
    return np.exp2(a.ravel()).repeat(32)


def f64(x):
    return np.asarray(x).astype(np.float64)


def striped(idx):
    return np.tile(idx.reshape(-1, 16).T, (8, 1)).astype(np.uint16)


def unstriped(offs):
    return offs[:16].T.reshape(-1).astype(np.int64)


def striped8(idx):
    return np.concatenate([v.reshape(-1, 16).T for v in idx]).astype(np.uint16)


def unstriped8(offs):
    return np.stack([offs[16 * g:16 * g + 16].T.reshape(-1) for g in range(8)]).astype(np.int64)


E2M1 = np.array([0.0, 0.5, 1.0, 1.5, 2.0, 3.0, 4.0, 6.0, -0.0, -0.5, -1.0, -1.5, -2.0, -3.0, -4.0, -6.0])


def pack_weight(w, fmt):
    k, n = w.shape
    w = f64(np.asarray(w, np.float32).astype(ml_dtypes.bfloat16)).reshape(k // 32, 32, n)
    amax = np.abs(w).max(1)
    if fmt == "e4m3":
        byte = np.frexp(amax)[1] - 1 + 127 - 7
    else:
        mant, ex = np.frexp(amax / 6.0)
        byte = np.where(mant > 0.5, ex, ex - 1) + 127
    byte = np.clip(np.where(amax > 0, byte, 1), 1, 254)
    scaled = (w * np.exp2(127.0 - byte)[:, None, :]).reshape(k, n).astype(np.float32)
    by_word = np.ascontiguousarray(scaled.reshape(k // 512, 128, 4, n).transpose(0, 1, 3, 2))
    if fmt == "e4m3":
        words = by_word.astype(ml_dtypes.float8_e4m3fn).view(np.uint8)
    else:
        c = by_word.astype(ml_dtypes.float4_e2m1fn).view(np.uint8) & 0xF
        words = (c[..., 0::2] | (c[..., 1::2] << 4)).reshape(k // 512, 128, 2 * n)
    return np.ascontiguousarray(words), np.ascontiguousarray(byte.astype(np.uint8).reshape(k // 512, 16, n))


def unpack_weight(words, scales, fmt):
    g, _, n = scales.shape
    words = np.ascontiguousarray(words).reshape(g, 128, n, -1)
    if fmt == "e4m3":
        vals = words.view(ml_dtypes.float8_e4m3fn).astype(np.float64)
    else:
        nib = np.empty((g, 128, n, 4), np.uint8)
        nib[..., 0::2] = words & 0xF
        nib[..., 1::2] = words >> 4
        vals = E2M1[nib]
    vals = vals * np.repeat(np.exp2(scales.astype(np.float64) - 127.0), 8, axis=1)[..., None]
    return vals.transpose(0, 1, 3, 2).reshape(g * 512, n)


def pack_table(v):
    words, scales = pack_weight(v, "e4m3")
    return np.concatenate([words.reshape(words.shape[0], -1), scales.reshape(scales.shape[0], -1)], axis=1)


def unpack_table(tab):
    g, t = tab.shape[0], tab.shape[1] // 528
    return unpack_weight(tab[:, :512 * t].reshape(g, 128, t, 4), tab[:, 512 * t:].reshape(g, 16, t), "e4m3")


K, L, M, T, S = 1024, 512, 128, 2048, 1024


def setup_inputs():
    n = np.random.standard_normal
    s1 = mx_kscale(K)[:, None]
    s2 = mx_kscale(L)[:, None]
    p_w4 = pack_weight(n((K, M)) / np.sqrt(K) / s1, "e2m1")
    return {
        "xT": (n((K, T)) * s1).astype(np.float32),
        "w4_words": p_w4[0],
        "w4_scales": p_w4[1],
        "tab": pack_table(n((L, T)) * s2),
        "u": (n((L, M)) / np.sqrt(L) / s2).astype(np.float32),
        "wgt": np.repeat(np.random.uniform(0.5, 2.0, (8, S)), 16, axis=0).astype(np.float32),
        "offs": striped(np.random.permutation(T)[:S]),
        "offs2": striped8(np.stack([np.random.permutation(T)[:S] for _ in range(8)])),
    }


def reference(xT, w4_words, w4_scales, tab, u, wgt, offs, offs2):
    idx2 = unstriped8(offs2)
    group = np.arange(K) % 512 // 64
    xg = f64(wgt)[np.arange(K) // 4 % 128] * f64(xT)[np.arange(K)[:, None], idx2[group]]
    xT_ = mxq(xg, 0, "e4m3")
    w4_ = unpack_weight(w4_words, w4_scales, "e2m1")
    tab_ = unpack_table(tab)[:, unstriped(offs)]
    u_ = mxq(f64(u), 0, "e4m3")
    y = xT_.T @ w4_ + tab_.T @ u_
    return y

@@ -1,0 +1,142 @@
+from contextlib import ExitStack
+
+import concourse.mybir as mybir
+
+K, L, M, T, S = 1024, 512, 128, 2048, 1024
+FLOPS = 2 * (K + L) * S * M
+
+F32 = mybir.dt.float32
+BF16 = mybir.dt.bfloat16
+I32 = mybir.dt.int32
+U32 = mybir.dt.uint32
+U16 = mybir.dt.uint16
+U8 = mybir.dt.uint8
+E4M3 = mybir.dt.float8_e4m3fn_x4
+E2M1 = mybir.dt.float4_e2m1fn_x4
+MULT = mybir.AluOpType.mult
+
+P = 128
+PACK = 4
+LIST_ROWS = 16
+
+
+def tile_list_htab_tm_none_kernel(tc, xT, w4_words, w4_scales, tab, u, wgt, offs, offs2, out):
+    nc = tc.nc
+    with ExitStack() as ctx:
+        pool = ctx.enter_context(tc.tile_pool(name="held", bufs=1))
+        psum = ctx.enter_context(tc.psum_pool(name="psum", bufs=1))
+
+        list1 = pool.tile([P, S // LIST_ROWS], U16, name="list1")
+        list8 = pool.tile([P, S // LIST_ROWS], U16, name="list8")
+        tab_scales = pool.tile([P, T], U8, name="tab_scales", align_bytes=64)
+        w4_sc = pool.tile([P, 2, M], U8, name="w4_sc", align_bytes=64)
+        v_scales = pool.tile([P, S], U8, name="v_scales", align_bytes=64)
+        for lo, hi in ((0, 16), (32, 64), (64, 128)):
+            nc.gpsimd.memset(tab_scales[lo:hi, :].bitcast(I32), 0)
+        nc.gpsimd.memset(w4_sc[:].bitcast(I32), 0)
+        nc.gpsimd.memset(v_scales[:].bitcast(I32), 0)
+
+        nc.sync.dma_start(list1[:], offs)
+        scale_rows = tab[0, 512 * T : 528 * T].rearrange("(r t) -> r t", t=T).bitcast(I32)
+        nc.sync.dma_start(tab_scales[16:32, :].bitcast(I32), scale_rows)
+        nc.sync.dma_start(list8[:], offs2)
+        for q in range(4):
+            nc.scalar.dma_start(
+                w4_sc[32 * q : 32 * q + 4, :, :].bitcast(I32),
+                w4_scales[:, 4 * q : 4 * q + 4, :].rearrange("a r n -> r a n").bitcast(I32),
+            )
+
+        planes = xT.rearrange("(a p i) t -> a i p t", a=2, i=PACK)
+        x_sb = [[pool.tile([P, T], F32, name="x_%d_%d" % (a, i)) for i in range(PACK)] for a in range(2)]
+        wgt_sb = pool.tile([P, S], F32, name="wgt_sb")
+        u_raw = pool.tile([P, PACK, M], F32, name="u_raw")
+        w4_sb = pool.tile([P, 2, 2 * M], U8, name="w4_sb", align_bytes=64)
+        tab_words = pool.tile([P, T], I32, name="tab_words")
+
+        H = S // 2
+        nc.sync.dma_start(wgt_sb[:, :H], wgt[:, :H])
+        nc.sync.dma_start(x_sb[0][0][:], planes[0, 0])
+        nc.sync.dma_start(wgt_sb[:, H:], wgt[:, H:])
+        for i in range(1, PACK):
+            nc.sync.dma_start(x_sb[0][i][:], planes[0, i])
+        nc.sync.dma_start(x_sb[1][0][:], planes[1, 0])
+        nc.sync.dma_start(x_sb[1][1][:], planes[1, 1])
+        nc.sync.dma_start(w4_sb[:].bitcast(I32), w4_words.rearrange("a p b -> p a b").bitcast(I32))
+        nc.sync.dma_start(u_raw[:], u.rearrange("(p i) n -> p i n", i=PACK))
+        nc.sync.dma_start(x_sb[1][2][:], planes[1, 2])
+        nc.sync.dma_start(x_sb[1][3][:], planes[1, 3])
+        nc.sync.dma_start(tab_words[:], tab[0, 0 : 512 * T].rearrange("(p b) -> p b", p=P).bitcast(I32))
+
+        def cols(lo, hi):
+            return slice(lo // LIST_ROWS, hi // LIST_ROWS)
+
+        v_rows = pool.tile([P, S], U8, name="v_rows", align_bytes=64)
+        nc.vector.tensor_copy(v_rows[:], tab_scales[:].indirect(list1[:]))
+        for q in range(4):
+            nc.scalar.dma_start(v_scales[32 * q : 32 * q + 4, :].bitcast(I32), v_rows[16 + 4 * q : 20 + 4 * q, :].bitcast(I32))
+
+        picked = [pool.tile([P, PACK, S], F32, name="picked_%d" % a) for a in range(2)]
+        woven = [pool.tile([P, S, PACK], BF16, name="woven_%d" % a, align_bytes=64) for a in range(2)]
+        x_codes = [pool.tile([P, S], U32, name="x_codes_%d" % a, align_bytes=64) for a in range(2)]
+        x_scales = [pool.tile([P, S], U8, name="x_scales_%d" % a, align_bytes=64) for a in range(2)]
+
+        def pick(a, i, lo, hi):
+            nc.vector.tensor_tensor(picked[a][:, i, lo:hi], x_sb[a][i][:].indirect(list8[:, cols(lo, hi)]), wgt_sb[:, lo:hi], MULT)
+
+        def weave(dst, src):
+            nc.scalar.copy(dst.rearrange("p (c e) i -> p c i e", e=4), src.rearrange("p i (c e) -> p c i e", e=4))
+
+        def quantise(codes, scales, src):
+            nc.vector.quantize_mx(out=codes.bitcast(E4M3), scales=scales, in_=src.rearrange("p s i -> p (s i)"))
+
+        acc = [psum.tile([P, M], F32, name="acc_%d" % b) for b in range(S // P)]
+
+        def head_pass(a, b):
+            js = slice(b * P, (b + 1) * P)
+            nc.tensor.matmul_mx(
+                out=acc[b][:], lhsT=x_codes[a][:, js].bitcast(E4M3), lhsT_scale=x_scales[a][:, js],
+                rhs=w4_sb[:, a, :].bitcast(E2M1), rhs_scale=w4_sc[:, a, :], start=(a == 0), stop=(a == 1))
+
+        pick(0, 0, 0, H)
+        pick(0, 0, H, S)
+        for i in range(1, PACK):
+            pick(0, i, 0, S)
+        weave(woven[0][:], picked[0][:])
+        pick(1, 0, 0, S)
+        pick(1, 1, 0, S)
+        quantise(x_codes[0][:], x_scales[0][:], woven[0][:])
+        for b in range(S // P):
+            head_pass(0, b)
+
+        u_woven = pool.tile([P, M, PACK], BF16, name="u_woven", align_bytes=64)
+        u_codes = pool.tile([P, M], U32, name="u_codes", align_bytes=64)
+        u_scales = pool.tile([P, M], U8, name="u_scales", align_bytes=64)
+        weave(u_woven[:], u_raw[:])
+        pick(1, 2, 0, S)
+        quantise(u_codes[:], u_scales[:], u_woven[:])
+
+        Q = S // 4
+        for c in range(4):
+            pick(1, 3, c * Q, (c + 1) * Q)
+            weave(woven[1][:, c * Q : (c + 1) * Q, :], picked[1][:, :, c * Q : (c + 1) * Q])
+
+        v_words = pool.tile([P, S], U32, name="v_words", align_bytes=64)
+        out_rows = out.rearrange("(b p) n -> p b n", p=P)
+        for c in range(4):
+            js = slice(c * Q, (c + 1) * Q)
+            nc.vector.tensor_copy(v_words[:, js], tab_words[:].bitcast(U32).indirect(list1[:, cols(c * Q, (c + 1) * Q)]))
+            for b in (2 * c, 2 * c + 1):
+                bs = slice(b * P, (b + 1) * P)
+                nc.tensor.matmul_mx(
+                    out=acc[b][:], lhsT=v_words[:, bs].bitcast(E4M3), lhsT_scale=v_scales[:, bs],
+                    rhs=u_codes[:].bitcast(E4M3), rhs_scale=u_scales[:], start=False, stop=False)
+            quantise(x_codes[1][:, js], x_scales[1][:, js], woven[1][:, js, :])
+            result = pool.tile([P, 2, M], F32, name="result_%d" % c)
+            for e in range(2):
+                head_pass(1, 2 * c + e)
+            nc.scalar.copy(result[:, 0, :], acc[2 * c][:])
+            if c == 3:
+                nc.vector.tensor_copy(result[:, 1, :], acc[2 * c + 1][:])
+            else:
+                nc.scalar.copy(result[:, 1, :], acc[2 * c + 1][:])
+            nc.sync.dma_start(out_rows[:, 2 * c : 2 * c + 2, :], result[:])

@@ -41,7 +41,7 @@ def tile_list_htab_tm_none_kernel(tc, xT, w4_words, w4_scales, tab, u, wgt, offs
         nc.sync.dma_start(tab_scales[16:32, :].bitcast(I32), scale_rows)
         nc.sync.dma_start(list8[:], offs2)
         for q in range(4):
-            nc.scalar.dma_start(
+            nc.gpsimd.dma_start(
                 w4_sc[32 * q : 32 * q + 4, :, :].bitcast(I32),
                 w4_scales[:, 4 * q : 4 * q + 4, :].rearrange("a r n -> r a n").bitcast(I32),
             )
@@ -73,7 +73,7 @@ def tile_list_htab_tm_none_kernel(tc, xT, w4_words, w4_scales, tab, u, wgt, offs
         v_rows = pool.tile([P, S], U8, name="v_rows", align_bytes=64)
         nc.vector.tensor_copy(v_rows[:], tab_scales[:].indirect(list1[:]))
         for q in range(4):
-            nc.scalar.dma_start(v_scales[32 * q : 32 * q + 4, :].bitcast(I32), v_rows[16 + 4 * q : 20 + 4 * q, :].bitcast(I32))
+            nc.gpsimd.dma_start(v_scales[32 * q : 32 * q + 4, :].bitcast(I32), v_rows[16 + 4 * q : 20 + 4 * q, :].bitcast(I32))
 
         picked = [pool.tile([P, PACK, S], F32, name="picked_%d" % a) for a in range(2)]
         woven = [pool.tile([P, S, PACK], BF16, name="woven_%d" % a, align_bytes=64) for a in range(2)]
@@ -99,14 +99,18 @@ def tile_list_htab_tm_none_kernel(tc, xT, w4_words, w4_scales, tab, u, wgt, offs
 
         pick(0, 0, 0, H)
         pick(0, 0, H, S)
-        for i in range(1, PACK):
-            pick(0, i, 0, S)
-        weave(woven[0][:], picked[0][:])
-        pick(1, 0, 0, S)
-        pick(1, 1, 0, S)
-        quantise(x_codes[0][:], x_scales[0][:], woven[0][:])
-        for b in range(S // P):
-            head_pass(0, b)
+        pick(0, 1, 0, S)
+        pick(0, 2, 0, S)
+        for h in range(2):
+            js = slice(h * H, (h + 1) * H)
+            pick(0, 3, h * H, (h + 1) * H)
+            weave(woven[0][:, js, :], picked[0][:, :, js])
+        for h in range(2):
+            js = slice(h * H, (h + 1) * H)
+            pick(1, h, 0, S)
+            quantise(x_codes[0][:, js], x_scales[0][:, js], woven[0][:, js, :])
+            for b in range(4 * h, 4 * h + 4):
+                head_pass(0, b)
 
         u_woven = pool.tile([P, M, PACK], BF16, name="u_woven", align_bytes=64)
         u_codes = pool.tile([P, M], U32, name="u_codes", align_bytes=64)

@@ -17,7 +17,14 @@ MULT = mybir.AluOpType.mult
 
 P = 128
 PACK = 4
-LIST_ROWS = 16
+PASSES = K // (P * PACK)
+GROUP = 16
+QUADRANT = 32
+SCALE_ROWS = 4
+BLOCKS = P * PACK // 32
+LINE = 4
+HALF = S // 2
+QUARTER = S // 4
 
 
 def tile_list_htab_tm_none_kernel(tc, xT, w4_words, w4_scales, tab, u, wgt, offs, offs2, out):
@@ -26,121 +33,140 @@ def tile_list_htab_tm_none_kernel(tc, xT, w4_words, w4_scales, tab, u, wgt, offs
         pool = ctx.enter_context(tc.tile_pool(name="held", bufs=1))
         psum = ctx.enter_context(tc.psum_pool(name="psum", bufs=1))
 
-        list1 = pool.tile([P, S // LIST_ROWS], U16, name="list1")
-        list8 = pool.tile([P, S // LIST_ROWS], U16, name="list8")
+        table_list = pool.tile([P, S // GROUP], U16, name="table_list")
+        head_lists = pool.tile([P, S // GROUP], U16, name="head_lists")
         tab_scales = pool.tile([P, T], U8, name="tab_scales", align_bytes=64)
-        w4_sc = pool.tile([P, 2, M], U8, name="w4_sc", align_bytes=64)
-        v_scales = pool.tile([P, S], U8, name="v_scales", align_bytes=64)
-        for lo, hi in ((0, 16), (32, 64), (64, 128)):
-            nc.gpsimd.memset(tab_scales[lo:hi, :].bitcast(I32), 0)
-        nc.gpsimd.memset(w4_sc[:].bitcast(I32), 0)
-        nc.gpsimd.memset(v_scales[:].bitcast(I32), 0)
+        w4_plane = pool.tile([P, PASSES, M], U8, name="w4_plane", align_bytes=64)
+        v_plane = pool.tile([P, S], U8, name="v_plane", align_bytes=64)
 
-        nc.sync.dma_start(list1[:], offs)
-        scale_rows = tab[0, 512 * T : 528 * T].rearrange("(r t) -> r t", t=T).bitcast(I32)
-        nc.sync.dma_start(tab_scales[16:32, :].bitcast(I32), scale_rows)
-        nc.sync.dma_start(list8[:], offs2)
-        for q in range(4):
-            nc.gpsimd.dma_start(
-                w4_sc[32 * q : 32 * q + 4, :, :].bitcast(I32),
-                w4_scales[:, 4 * q : 4 * q + 4, :].rearrange("a r n -> r a n").bitcast(I32),
-            )
+        for lo, hi in ((0, BLOCKS), (2 * BLOCKS, P // 2), (P // 2, P)):
+            nc.vector.memset(tab_scales[lo:hi, :].bitcast(I32), 0)
+        nc.vector.memset(w4_plane[:].bitcast(I32), 0)
+        nc.vector.memset(v_plane[:].bitcast(I32), 0)
 
-        planes = xT.rearrange("(a p i) t -> a i p t", a=2, i=PACK)
-        x_sb = [[pool.tile([P, T], F32, name="x_%d_%d" % (a, i)) for i in range(PACK)] for a in range(2)]
+        nc.sync.dma_start(table_list[:], offs)
+        scale_rows = tab[0, L * T : (L + BLOCKS) * T].rearrange("(q t) -> q t", t=T).bitcast(I32)
+        nc.sync.dma_start(tab_scales[BLOCKS : 2 * BLOCKS, :].bitcast(I32), scale_rows)
+        nc.sync.dma_start(head_lists[:], offs2)
+
+        x_rows = xT.rearrange("(a p i) t -> a i p t", a=PASSES, i=PACK)
+        planes = [[pool.tile([P, T], F32, name="plane_%d_%d" % (a, i)) for i in range(PACK)] for a in range(PASSES)]
         wgt_sb = pool.tile([P, S], F32, name="wgt_sb")
         u_raw = pool.tile([P, PACK, M], F32, name="u_raw")
-        w4_sb = pool.tile([P, 2, 2 * M], U8, name="w4_sb", align_bytes=64)
+        w4_codes = pool.tile([P, PASSES, 2 * M], U8, name="w4_codes", align_bytes=64)
         tab_words = pool.tile([P, T], I32, name="tab_words")
 
-        H = S // 2
-        nc.sync.dma_start(wgt_sb[:, :H], wgt[:, :H])
-        nc.sync.dma_start(x_sb[0][0][:], planes[0, 0])
-        nc.sync.dma_start(wgt_sb[:, H:], wgt[:, H:])
-        for i in range(1, PACK):
-            nc.sync.dma_start(x_sb[0][i][:], planes[0, i])
-        nc.sync.dma_start(x_sb[1][0][:], planes[1, 0])
-        nc.sync.dma_start(x_sb[1][1][:], planes[1, 1])
-        nc.sync.dma_start(w4_sb[:].bitcast(I32), w4_words.rearrange("a p b -> p a b").bitcast(I32))
-        nc.sync.dma_start(u_raw[:], u.rearrange("(p i) n -> p i n", i=PACK))
-        nc.sync.dma_start(x_sb[1][2][:], planes[1, 2])
-        nc.sync.dma_start(x_sb[1][3][:], planes[1, 3])
-        nc.sync.dma_start(tab_words[:], tab[0, 0 : 512 * T].rearrange("(p b) -> p b", p=P).bitcast(I32))
+        def load_plane(a, i):
+            nc.sync.dma_start(planes[a][i][:], x_rows[a, i])
 
-        def cols(lo, hi):
-            return slice(lo // LIST_ROWS, hi // LIST_ROWS)
+        nc.sync.dma_start(wgt_sb[:, :HALF], wgt[:, :HALF])
+        load_plane(0, 0)
+        nc.sync.dma_start(wgt_sb[:, HALF:], wgt[:, HALF:])
+        for i in range(1, PACK):
+            load_plane(0, i)
 
         v_rows = pool.tile([P, S], U8, name="v_rows", align_bytes=64)
-        nc.vector.tensor_copy(v_rows[:], tab_scales[:].indirect(list1[:]))
-        for q in range(4):
-            nc.gpsimd.dma_start(v_scales[32 * q : 32 * q + 4, :].bitcast(I32), v_rows[16 + 4 * q : 20 + 4 * q, :].bitcast(I32))
+        nc.vector.tensor_copy(v_rows[:], tab_scales[:].indirect(table_list[:]))
 
-        picked = [pool.tile([P, PACK, S], F32, name="picked_%d" % a) for a in range(2)]
-        woven = [pool.tile([P, S, PACK], BF16, name="woven_%d" % a, align_bytes=64) for a in range(2)]
-        x_codes = [pool.tile([P, S], U32, name="x_codes_%d" % a, align_bytes=64) for a in range(2)]
-        x_scales = [pool.tile([P, S], U8, name="x_scales_%d" % a, align_bytes=64) for a in range(2)]
+        load_plane(1, 0)
+        load_plane(1, 1)
+        nc.sync.dma_start(w4_codes[:].bitcast(I32), w4_words.rearrange("a p b -> p a b").bitcast(I32))
+        nc.sync.dma_start(u_raw[:], u.rearrange("(p i) n -> p i n", i=PACK))
+        load_plane(1, 2)
+        load_plane(1, 3)
+        nc.sync.dma_start(tab_words[:], tab[0, 0 : L * T].rearrange("(p b) -> p b", p=P).bitcast(I32))
+
+        for q in range(P // QUADRANT):
+            nc.sync.dma_start(
+                w4_plane[QUADRANT * q : QUADRANT * q + SCALE_ROWS, :, :].bitcast(I32),
+                w4_scales[:, SCALE_ROWS * q : SCALE_ROWS * (q + 1), :].rearrange("a r n -> r a n").bitcast(I32),
+            )
+        for q in range(P // QUADRANT):
+            nc.sync.dma_start(
+                v_plane[QUADRANT * q : QUADRANT * q + SCALE_ROWS, :].bitcast(I32),
+                v_rows[BLOCKS + SCALE_ROWS * q : BLOCKS + SCALE_ROWS * (q + 1), :].bitcast(I32),
+            )
+
+        picked = [pool.tile([P, PACK, S], F32, name="picked_%d" % a) for a in range(PASSES)]
+        woven = [pool.tile([P, S, PACK], BF16, name="woven_%d" % a, align_bytes=64) for a in range(PASSES)]
+        first_codes = pool.tile([P, S], U32, name="first_codes", align_bytes=64)
+        x_planes = [pool.tile([P, S], U8, name="x_plane_%d" % a, align_bytes=64) for a in range(PASSES)]
+
+        def entries(lo, hi):
+            return slice(lo // GROUP, hi // GROUP)
 
         def pick(a, i, lo, hi):
-            nc.vector.tensor_tensor(picked[a][:, i, lo:hi], x_sb[a][i][:].indirect(list8[:, cols(lo, hi)]), wgt_sb[:, lo:hi], MULT)
+            window = planes[a][i][:].indirect(head_lists[:, entries(lo, hi)])
+            nc.vector.tensor_tensor(picked[a][:, i, lo:hi], window, wgt_sb[:, lo:hi], MULT)
 
         def weave(dst, src):
-            nc.scalar.copy(dst.rearrange("p (c e) i -> p c i e", e=4), src.rearrange("p i (c e) -> p c i e", e=4))
+            nc.scalar.copy(dst.rearrange("p (c e) i -> p c i e", e=LINE), src.rearrange("p i (c e) -> p c i e", e=LINE))
+
+        def weave_pair(dst, src):
+            nc.scalar.copy(dst, src.rearrange("p i s -> p s i"))
 
         def quantise(codes, scales, src):
             nc.vector.quantize_mx(out=codes.bitcast(E4M3), scales=scales, in_=src.rearrange("p s i -> p (s i)"))
 
         acc = [psum.tile([P, M], F32, name="acc_%d" % b) for b in range(S // P)]
 
-        def head_pass(a, b):
-            js = slice(b * P, (b + 1) * P)
+        def multiply(b, codes, plane, weights, weight_plane, start, stop):
             nc.tensor.matmul_mx(
-                out=acc[b][:], lhsT=x_codes[a][:, js].bitcast(E4M3), lhsT_scale=x_scales[a][:, js],
-                rhs=w4_sb[:, a, :].bitcast(E2M1), rhs_scale=w4_sc[:, a, :], start=(a == 0), stop=(a == 1))
+                out=acc[b][:],
+                lhsT=codes.bitcast(E4M3),
+                lhsT_scale=plane[:, b * P : (b + 1) * P],
+                rhs=weights,
+                rhs_scale=weight_plane,
+                start=start,
+                stop=stop,
+            )
 
-        pick(0, 0, 0, H)
-        pick(0, 0, H, S)
+        pick(0, 0, 0, HALF)
+        pick(0, 0, HALF, S)
         pick(0, 1, 0, S)
         pick(0, 2, 0, S)
+        for lo in (0, HALF):
+            pick(0, 3, lo, lo + HALF)
+            weave(woven[0][:, lo : lo + HALF, :], picked[0][:, :, lo : lo + HALF])
         for h in range(2):
-            js = slice(h * H, (h + 1) * H)
-            pick(0, 3, h * H, (h + 1) * H)
-            weave(woven[0][:, js, :], picked[0][:, :, js])
-        for h in range(2):
-            js = slice(h * H, (h + 1) * H)
+            lo = h * HALF
             pick(1, h, 0, S)
-            quantise(x_codes[0][:, js], x_scales[0][:, js], woven[0][:, js, :])
-            for b in range(4 * h, 4 * h + 4):
-                head_pass(0, b)
+            quantise(first_codes[:, lo : lo + HALF], x_planes[0][:, lo : lo + HALF], woven[0][:, lo : lo + HALF, :])
+            for b in range(lo // P, (lo + HALF) // P):
+                codes = first_codes[:, b * P : (b + 1) * P]
+                multiply(b, codes, x_planes[0], w4_codes[:, 0, :].bitcast(E2M1), w4_plane[:, 0, :], True, False)
 
         u_woven = pool.tile([P, M, PACK], BF16, name="u_woven", align_bytes=64)
         u_codes = pool.tile([P, M], U32, name="u_codes", align_bytes=64)
-        u_scales = pool.tile([P, M], U8, name="u_scales", align_bytes=64)
+        u_plane = pool.tile([P, M], U8, name="u_plane", align_bytes=64)
         weave(u_woven[:], u_raw[:])
+        weave_pair(woven[1][:, :, 0:2], picked[1][:, 0:2, :])
         pick(1, 2, 0, S)
-        quantise(u_codes[:], u_scales[:], u_woven[:])
+        quantise(u_codes[:], u_plane[:], u_woven[:])
+        for half_lo in (0, HALF):
+            pick(1, 3, half_lo, half_lo + HALF)
+            for lo in (half_lo, half_lo + QUARTER):
+                weave_pair(woven[1][:, lo : lo + QUARTER, 2:4], picked[1][:, 2:4, lo : lo + QUARTER])
 
-        Q = S // 4
-        for c in range(4):
-            pick(1, 3, c * Q, (c + 1) * Q)
-            weave(woven[1][:, c * Q : (c + 1) * Q, :], picked[1][:, :, c * Q : (c + 1) * Q])
-
-        v_words = pool.tile([P, S], U32, name="v_words", align_bytes=64)
         out_rows = out.rearrange("(b p) n -> p b n", p=P)
-        for c in range(4):
-            js = slice(c * Q, (c + 1) * Q)
-            nc.vector.tensor_copy(v_words[:, js], tab_words[:].bitcast(U32).indirect(list1[:, cols(c * Q, (c + 1) * Q)]))
-            for b in (2 * c, 2 * c + 1):
-                bs = slice(b * P, (b + 1) * P)
-                nc.tensor.matmul_mx(
-                    out=acc[b][:], lhsT=v_words[:, bs].bitcast(E4M3), lhsT_scale=v_scales[:, bs],
-                    rhs=u_codes[:].bitcast(E4M3), rhs_scale=u_scales[:], start=False, stop=False)
-            quantise(x_codes[1][:, js], x_scales[1][:, js], woven[1][:, js, :])
-            result = pool.tile([P, 2, M], F32, name="result_%d" % c)
-            for e in range(2):
-                head_pass(1, 2 * c + e)
-            nc.scalar.copy(result[:, 0, :], acc[2 * c][:])
-            if c == 3:
-                nc.vector.tensor_copy(result[:, 1, :], acc[2 * c + 1][:])
+        for lo in range(0, S, QUARTER):
+            tiles = (lo // P, lo // P + 1)
+            slot = "quarter_%d" % (lo // QUARTER)
+            v_words = pool.tile([P, QUARTER], U32, name="v_words", tag=slot, align_bytes=64)
+            nc.vector.tensor_copy(v_words[:], tab_words[:].bitcast(U32).indirect(table_list[:, entries(lo, lo + QUARTER)]))
+            for e, b in enumerate(tiles):
+                multiply(b, v_words[:, e * P : (e + 1) * P], v_plane, u_codes[:].bitcast(E4M3), u_plane[:], False, False)
+
+            last_codes = pool.tile([P, QUARTER], U32, name="last_codes", tag=slot, align_bytes=64)
+            quantise(last_codes[:], x_planes[1][:, lo : lo + QUARTER], woven[1][:, lo : lo + QUARTER, :])
+            for e, b in enumerate(tiles):
+                codes = last_codes[:, e * P : (e + 1) * P]
+                multiply(b, codes, x_planes[1], w4_codes[:, 1, :].bitcast(E2M1), w4_plane[:, 1, :], False, True)
+
+            result = pool.tile([P, len(tiles), M], F32, name="result_%d" % (lo // QUARTER))
+            nc.scalar.copy(result[:, 0, :], acc[tiles[0]][:])
+            if lo + QUARTER == S:
+                nc.vector.tensor_copy(result[:, 1, :], acc[tiles[1]][:])
             else:
-                nc.scalar.copy(result[:, 1, :], acc[2 * c + 1][:])
-            nc.sync.dma_start(out_rows[:, 2 * c : 2 * c + 2, :], result[:])
+                nc.scalar.copy(result[:, 1, :], acc[tiles[1]][:])
+            nc.sync.dma_start(out_rows[:, tiles[0] : tiles[1] + 1, :], result[:])

from contextlib import ExitStack

import concourse.mybir as mybir

K, L, M, T, S = 1024, 512, 128, 2048, 1024
FLOPS = 2 * (K + L) * S * M

F32 = mybir.dt.float32
BF16 = mybir.dt.bfloat16
I32 = mybir.dt.int32
U32 = mybir.dt.uint32
U16 = mybir.dt.uint16
U8 = mybir.dt.uint8
E4M3 = mybir.dt.float8_e4m3fn_x4
E2M1 = mybir.dt.float4_e2m1fn_x4
MULT = mybir.AluOpType.mult

P = 128
PACK = 4
PASSES = K // (P * PACK)
GROUP = 16
QUADRANT = 32
SCALE_ROWS = 4
BLOCKS = P * PACK // 32
LINE = 4
HALF = S // 2
QUARTER = S // 4


def tile_list_htab_tm_none_kernel(tc, xT, w4_words, w4_scales, tab, u, wgt, offs, offs2, out):
    nc = tc.nc
    with ExitStack() as ctx:
        pool = ctx.enter_context(tc.tile_pool(name="held", bufs=1))
        psum = ctx.enter_context(tc.psum_pool(name="psum", bufs=1))

        table_list = pool.tile([P, S // GROUP], U16, name="table_list")
        head_lists = pool.tile([P, S // GROUP], U16, name="head_lists")
        tab_scales = pool.tile([P, T], U8, name="tab_scales", align_bytes=64)
        w4_plane = pool.tile([P, PASSES, M], U8, name="w4_plane", align_bytes=64)
        v_plane = pool.tile([P, S], U8, name="v_plane", align_bytes=64)

        for lo, hi in ((0, BLOCKS), (2 * BLOCKS, P // 2), (P // 2, P)):
            nc.vector.memset(tab_scales[lo:hi, :].bitcast(I32), 0)
        nc.vector.memset(w4_plane[:].bitcast(I32), 0)
        nc.vector.memset(v_plane[:].bitcast(I32), 0)

        nc.sync.dma_start(table_list[:], offs)
        scale_rows = tab[0, L * T : (L + BLOCKS) * T].rearrange("(q t) -> q t", t=T).bitcast(I32)
        nc.sync.dma_start(tab_scales[BLOCKS : 2 * BLOCKS, :].bitcast(I32), scale_rows)
        nc.sync.dma_start(head_lists[:], offs2)

        x_rows = xT.rearrange("(a p i) t -> a i p t", a=PASSES, i=PACK)
        planes = [[pool.tile([P, T], F32, name="plane_%d_%d" % (a, i)) for i in range(PACK)] for a in range(PASSES)]
        wgt_sb = pool.tile([P, S], F32, name="wgt_sb")
        u_raw = pool.tile([P, PACK, M], F32, name="u_raw")
        w4_codes = pool.tile([P, PASSES, 2 * M], U8, name="w4_codes", align_bytes=64)
        tab_words = pool.tile([P, T], I32, name="tab_words")

        def load_plane(a, i):
            nc.sync.dma_start(planes[a][i][:], x_rows[a, i])

        nc.sync.dma_start(wgt_sb[:, :HALF], wgt[:, :HALF])
        load_plane(0, 0)
        nc.sync.dma_start(wgt_sb[:, HALF:], wgt[:, HALF:])
        for i in range(1, PACK):
            load_plane(0, i)

        v_rows = pool.tile([P, S], U8, name="v_rows", align_bytes=64)
        nc.vector.tensor_copy(v_rows[:], tab_scales[:].indirect(table_list[:]))

        load_plane(1, 0)
        load_plane(1, 1)
        nc.sync.dma_start(w4_codes[:].bitcast(I32), w4_words.rearrange("a p b -> p a b").bitcast(I32))
        nc.sync.dma_start(u_raw[:], u.rearrange("(p i) n -> p i n", i=PACK))
        load_plane(1, 2)
        load_plane(1, 3)
        nc.sync.dma_start(tab_words[:], tab[0, 0 : L * T].rearrange("(p b) -> p b", p=P).bitcast(I32))

        for q in range(P // QUADRANT):
            nc.sync.dma_start(
                w4_plane[QUADRANT * q : QUADRANT * q + SCALE_ROWS, :, :].bitcast(I32),
                w4_scales[:, SCALE_ROWS * q : SCALE_ROWS * (q + 1), :].rearrange("a r n -> r a n").bitcast(I32),
            )
        for q in range(P // QUADRANT):
            nc.sync.dma_start(
                v_plane[QUADRANT * q : QUADRANT * q + SCALE_ROWS, :].bitcast(I32),
                v_rows[BLOCKS + SCALE_ROWS * q : BLOCKS + SCALE_ROWS * (q + 1), :].bitcast(I32),
            )

        picked = [pool.tile([P, PACK, S], F32, name="picked_%d" % a) for a in range(PASSES)]
        woven = [pool.tile([P, S, PACK], BF16, name="woven_%d" % a, align_bytes=64) for a in range(PASSES)]
        first_codes = pool.tile([P, S], U32, name="first_codes", align_bytes=64)
        x_planes = [pool.tile([P, S], U8, name="x_plane_%d" % a, align_bytes=64) for a in range(PASSES)]

        def entries(lo, hi):
            return slice(lo // GROUP, hi // GROUP)

        def pick(a, i, lo, hi):
            window = planes[a][i][:].indirect(head_lists[:, entries(lo, hi)])
            nc.vector.tensor_tensor(picked[a][:, i, lo:hi], window, wgt_sb[:, lo:hi], MULT)

        def weave(dst, src):
            nc.scalar.copy(dst.rearrange("p (c e) i -> p c i e", e=LINE), src.rearrange("p i (c e) -> p c i e", e=LINE))

        def weave_pair(dst, src):
            nc.scalar.copy(dst, src.rearrange("p i s -> p s i"))

        def quantise(codes, scales, src):
            nc.vector.quantize_mx(out=codes.bitcast(E4M3), scales=scales, in_=src.rearrange("p s i -> p (s i)"))

        acc = [psum.tile([P, M], F32, name="acc_%d" % b) for b in range(S // P)]

        def multiply(b, codes, plane, weights, weight_plane, start, stop):
            nc.tensor.matmul_mx(
                out=acc[b][:],
                lhsT=codes.bitcast(E4M3),
                lhsT_scale=plane[:, b * P : (b + 1) * P],
                rhs=weights,
                rhs_scale=weight_plane,
                start=start,
                stop=stop,
            )

        pick(0, 0, 0, HALF)
        pick(0, 0, HALF, S)
        pick(0, 1, 0, S)
        pick(0, 2, 0, S)
        for lo in (0, HALF):
            pick(0, 3, lo, lo + HALF)
            weave(woven[0][:, lo : lo + HALF, :], picked[0][:, :, lo : lo + HALF])
        for h in range(2):
            lo = h * HALF
            pick(1, h, 0, S)
            quantise(first_codes[:, lo : lo + HALF], x_planes[0][:, lo : lo + HALF], woven[0][:, lo : lo + HALF, :])
            for b in range(lo // P, (lo + HALF) // P):
                codes = first_codes[:, b * P : (b + 1) * P]
                multiply(b, codes, x_planes[0], w4_codes[:, 0, :].bitcast(E2M1), w4_plane[:, 0, :], True, False)

        u_woven = pool.tile([P, M, PACK], BF16, name="u_woven", align_bytes=64)
        u_codes = pool.tile([P, M], U32, name="u_codes", align_bytes=64)
        u_plane = pool.tile([P, M], U8, name="u_plane", align_bytes=64)
        weave(u_woven[:], u_raw[:])
        weave_pair(woven[1][:, :, 0:2], picked[1][:, 0:2, :])
        pick(1, 2, 0, S)
        quantise(u_codes[:], u_plane[:], u_woven[:])
        for half_lo in (0, HALF):
            pick(1, 3, half_lo, half_lo + HALF)
            for lo in (half_lo, half_lo + QUARTER):
                weave_pair(woven[1][:, lo : lo + QUARTER, 2:4], picked[1][:, 2:4, lo : lo + QUARTER])

        out_rows = out.rearrange("(b p) n -> p b n", p=P)
        for lo in range(0, S, QUARTER):
            tiles = (lo // P, lo // P + 1)
            slot = "quarter_%d" % (lo // QUARTER)
            v_words = pool.tile([P, QUARTER], U32, name="v_words", tag=slot, align_bytes=64)
            nc.vector.tensor_copy(v_words[:], tab_words[:].bitcast(U32).indirect(table_list[:, entries(lo, lo + QUARTER)]))
            for e, b in enumerate(tiles):
                multiply(b, v_words[:, e * P : (e + 1) * P], v_plane, u_codes[:].bitcast(E4M3), u_plane[:], False, False)

            last_codes = pool.tile([P, QUARTER], U32, name="last_codes", tag=slot, align_bytes=64)
            quantise(last_codes[:], x_planes[1][:, lo : lo + QUARTER], woven[1][:, lo : lo + QUARTER, :])
            for e, b in enumerate(tiles):
                codes = last_codes[:, e * P : (e + 1) * P]
                multiply(b, codes, x_planes[1], w4_codes[:, 1, :].bitcast(E2M1), w4_plane[:, 1, :], False, True)

            result = pool.tile([P, len(tiles), M], F32, name="result_%d" % (lo // QUARTER))
            nc.scalar.copy(result[:, 0, :], acc[tiles[0]][:])
            if lo + QUARTER == S:
                nc.vector.tensor_copy(result[:, 1, :], acc[tiles[1]][:])
            else:
                nc.scalar.copy(result[:, 1, :], acc[tiles[1]][:])
            nc.sync.dma_start(out_rows[:, tiles[0] : tiles[1] + 1, :], result[:])
